import numpy as np
import ml_dtypes


def mxq(x, axis, fmt="e4m3"):
    dtype, down = {"e4m3": (ml_dtypes.float8_e4m3fn, 7), "e5m2": (ml_dtypes.float8_e5m2, 14)}[fmt]
    v = np.moveaxis(np.asarray(x, np.float32).astype(ml_dtypes.bfloat16).astype(np.float64), axis, -1)
    blocks = v.reshape(v.shape[:-1] + (-1, 32))
    amax = np.abs(blocks).max(-1, keepdims=True)
    byte = np.maximum(np.where(amax > 0, np.frexp(amax)[1] - 1 + 127, 0) - down, 1)
    scale = np.exp2(byte - 127.0)
    codes = (blocks / scale).astype(np.float32).astype(dtype).astype(np.float64)
    return np.moveaxis((codes * scale).reshape(v.shape), -1, axis)


WIDE = False


def mx_kscale(k):
    if not WIDE:
        return np.ones(k)
    levels = np.array([10, -10, 5, -5, 0])
    if k % 512:
        return np.exp2(np.random.permutation(np.resize(levels, k // 32))).repeat(32)
    a = np.empty((k // 512, 16))
    for p in range(k // 512):
        a[p, :8] = np.random.permutation(np.resize(levels, 8))
        for g in range(8):
            far = levels[np.abs(levels - a[p, g]) >= 10]
            a[p, g + 8] = far[np.random.randint(len(far))]
    return np.exp2(a.ravel()).repeat(32)


def f64(x):
    return np.asarray(x).astype(np.float64)


def striped8(idx):
    return np.concatenate([x.reshape(-1, 16).T for x in idx]).astype(np.uint16)


def runs(offs, k):
    lists = np.stack([offs[16 * r : 16 * r + 16].T.reshape(-1) for r in range(8)]).astype(np.int64)
    return lists[np.arange(k) % 512 // 64]


def pack_weight(w):
    k, n = w.shape
    w = f64(np.asarray(w, np.float32).astype(ml_dtypes.bfloat16)).reshape(k // 32, 32, n)
    amax = np.abs(w).max(1)
    byte = np.clip(np.where(amax > 0, np.frexp(amax)[1] - 1 + 127 - 7, 1), 1, 254)
    scaled = (w * np.exp2(127.0 - byte)[:, None, :]).reshape(k, n).astype(np.float32)
    words = np.ascontiguousarray(scaled.reshape(k // 512, 128, 4, n).transpose(0, 1, 3, 2)).astype(ml_dtypes.float8_e4m3fn).view(np.uint8)
    return words, np.ascontiguousarray(byte.astype(np.uint8).reshape(k // 512, 16, n))


def unpack_weight(words, scales):
    g, p, n, _ = words.shape
    vals = np.ascontiguousarray(words).view(ml_dtypes.float8_e4m3fn).astype(np.float64) * np.repeat(np.exp2(scales.astype(np.float64) - 127.0), 8, axis=1)[..., None]
    return vals.transpose(0, 1, 3, 2).reshape(g * 512, n)


K, T, S, V, H = 512, 2048, 512, 512, 512


def setup_inputs():
    n = np.random.standard_normal
    s = mx_kscale(K)[:, None]
    packed_xT = pack_weight(n((K, T)) * s)
    return {
        "x_words": packed_xT[0],
        "x_scales": packed_xT[1],
        "w1": (n((K, H)) / np.sqrt(K) / s).astype(np.float32),
        "gs": (np.random.uniform(0.5, 1.5, (K, 1)) / s).astype(np.float32),
        "offs": striped8(np.random.randint(0, T, (8, S))),
        "cand": striped8(np.random.randint(0, T, (8, V))),
    }


def reference(x_words, x_scales, w1, gs, offs, cand):
    x_cand = unpack_weight(x_words, x_scales)[np.arange(K)[:, None], runs(cand, K)]
    xq = unpack_weight(x_words, x_scales)[np.arange(K)[:, None], runs(offs, K)]
    h = np.tanh(mxq(f64(w1), 0, "e4m3").T @ xq)
    z = f64(gs) * h
    return 0.0625 * ((x_cand.T @ mxq(z, 0, "e4m3")))

@@ -1,0 +1,139 @@
+from contextlib import ExitStack
+
+import concourse.mybir as mybir
+
+K, T, S, V, H = 512, 2048, 512, 512, 512
+FLOPS = 2 * K * H * S + 2 * K * V * S
+
+F32 = mybir.dt.float32
+BF16 = mybir.dt.bfloat16
+I32 = mybir.dt.int32
+U32 = mybir.dt.uint32
+U16 = mybir.dt.uint16
+U8 = mybir.dt.uint8
+FP8X4 = mybir.dt.float8_e4m3fn_x4
+ACT = mybir.ActivationFunctionType
+MULT = mybir.AluOpType.mult
+
+P = 128
+PACK = 4
+CHUNK = 128
+HALF = 256
+M_ON_SCALAR = 80
+OUT_SCALE = 0.0625
+
+
+def tile_picked_candhash_tanh_p_kernel(tc, x_words, x_scales, w1, gs, offs, cand, out):
+    nc = tc.nc
+    with ExitStack() as ctx:
+        keep = ctx.enter_context(tc.tile_pool(name="keep", bufs=1))
+        psum = ctx.enter_context(tc.psum_pool(name="psum", bufs=1))
+
+        offs_list = keep.tile([P, S // 16], U16, name="offs_list")
+        cand_list = keep.tile([P, V // 16], U16, name="cand_list")
+        table_words = keep.tile([P, T], U32, name="table_words")
+        table_scales = keep.tile([P, T], U8, name="table_scales")
+        w_raw = keep.tile([P, PACK, H], F32, name="w_raw")
+        gain = keep.tile([P, PACK], F32, name="gain")
+
+        nc.vector.memset(table_scales[:].bitcast(I32), 0)
+        nc.scalar.dma_start(out=w_raw[:], in_=w1.rearrange("(p j) c -> p j c", j=PACK))
+        nc.scalar.dma_start(out=table_words[:].bitcast(I32), in_=x_words[0].rearrange("p n t -> p (n t)").bitcast(I32))
+        nc.sync.dma_start(offs_list[:], offs)
+        scale_rows = x_scales[0].rearrange("(run r) n -> r run n", r=2)
+        for r in range(2):
+            nc.sync.dma_start(out=table_scales[r:P:16, :].bitcast(I32), in_=scale_rows[r].bitcast(I32))
+        nc.sync.dma_start(cand_list[:], cand)
+        nc.sync.dma_start(out=gain[:], in_=gs.rearrange("(p t) o -> p (t o)", t=PACK))
+
+        def picked_scales(index_list, label):
+            gathered = keep.tile([P, S], U8, name=label + "_gathered")
+            plane = keep.tile([P, S], U8, name=label + "_plane", align_bytes=64)
+            nc.vector.tensor_copy(gathered[:], table_scales[:].indirect(index_list[:]))
+            nc.vector.tensor_copy(plane[:].bitcast(I32), gathered[:].bitcast(I32))
+            for r in range(2):
+                nc.sync.dma_start(out=plane[2 + r : P : 32, :].bitcast(I32), in_=gathered[16 + r : P : 32, :].bitcast(I32))
+            return plane
+
+        def picked_words(index_list, half, label):
+            words = keep.tile([P, HALF], U32, name="%s_words%d" % (label, half), align_bytes=64)
+            cols = HALF // 16
+            nc.vector.tensor_copy(words[:], table_words[:].indirect(index_list[:, half * cols : (half + 1) * cols]))
+            return words
+
+        place_scales = picked_scales(offs_list, "place")
+        cand_scales = picked_scales(cand_list, "cand")
+
+        w_grouped = keep.tile([P, PACK, P, PACK], BF16, name="w_grouped", align_bytes=64)
+        w_dst = w_grouped[:].rearrange("p t m j -> p m j t")
+        w_src = w_raw[:].rearrange("p j (m t) -> p m j t", t=PACK)
+        nc.scalar.copy(out=w_dst[:, :M_ON_SCALAR], in_=w_src[:, :M_ON_SCALAR])
+        nc.vector.tensor_copy(out=w_dst[:, M_ON_SCALAR:], in_=w_src[:, M_ON_SCALAR:])
+        w_codes = keep.tile([P, H], U32, name="w_codes", align_bytes=64)
+        w_scales = keep.tile([P, H], U8, name="w_scales", align_bytes=64)
+        nc.vector.quantize_mx(out=w_codes[:].bitcast(FP8X4), scales=w_scales[:], in_=w_grouped[:].rearrange("p t m j -> p (t m j)"))
+
+        n_chunks = S // CHUNK
+        hidden = []
+        for half in range(2):
+            place_words = picked_words(offs_list, half, "place")
+            for c in range(half * 2, half * 2 + 2):
+                acc = psum.tile([P, PACK, CHUNK], F32, name="h_acc%d" % c, tag="h_acc%d" % c)
+                local = (c % 2) * CHUNK
+                for t in range(PACK):
+                    nc.tensor.matmul_mx(
+                        out=acc[:, t, :],
+                        lhsT=w_codes[:, t * P : (t + 1) * P].bitcast(FP8X4),
+                        lhsT_scale=w_scales[:, t * P : (t + 1) * P],
+                        rhs=place_words[:, local : local + CHUNK].bitcast(FP8X4),
+                        rhs_scale=place_scales[:, c * CHUNK : (c + 1) * CHUNK],
+                        start=True,
+                        stop=True,
+                    )
+                h = keep.tile([P, CHUNK, PACK], F32, name="h%d" % c)
+                nc.scalar.activation(out=h[:], in_=acc[:].rearrange("p t j -> p j t"), func=ACT.Tanh)
+                hidden.append(h)
+
+        cand_words = [picked_words(cand_list, half, "cand") for half in range(2)]
+        out_view = out.rearrange("(i p) j -> p i j", p=P)
+
+        def weigh(c):
+            z = keep.tile([P, CHUNK, PACK], BF16, name="z%d" % c, align_bytes=64)
+            nc.vector.tensor_tensor(out=z[:], in0=hidden[c][:], in1=gain[:].unsqueeze(1).to_broadcast([P, CHUNK, PACK]), op=MULT)
+            return z
+
+        def score(c, z):
+            z_codes = keep.tile([P, CHUNK], U32, name="z_codes%d" % c, align_bytes=64)
+            z_scales = keep.tile([P, CHUNK], U8, name="z_scales%d" % c, align_bytes=64)
+            nc.vector.quantize_mx(out=z_codes[:].bitcast(FP8X4), scales=z_scales[:], in_=z[:].rearrange("p j t -> p (j t)"))
+            last = c == n_chunks - 1
+            groups = [(0, 2), (2, 4)] if last else [(0, 4)]
+            for g, (i0, i1) in enumerate(groups):
+                tag = "h_acc0" if g == 1 else "o_acc%d" % c
+                acc = psum.tile([P, i1 - i0, CHUNK], F32, name="o_acc%d_%d" % (c, g), tag=tag)
+                for i in range(i0, i1):
+                    local = (i % 2) * P
+                    nc.tensor.matmul_mx(
+                        out=acc[:, i - i0, :],
+                        lhsT=cand_words[i // 2][:, local : local + P].bitcast(FP8X4),
+                        lhsT_scale=cand_scales[:, i * P : (i + 1) * P],
+                        rhs=z_codes[:].bitcast(FP8X4),
+                        rhs_scale=z_scales[:],
+                        start=True,
+                        stop=True,
+                    )
+                staged = keep.tile([P, i1 - i0, CHUNK], F32, name="staged%d_%d" % (c, g))
+                dst = out_view[:, i0:i1, c * CHUNK : (c + 1) * CHUNK]
+                if g == 1:
+                    nc.vector.tensor_scalar_mul(out=staged[:], in0=acc[:], scalar1=OUT_SCALE)
+                    nc.sync.dma_start(out=dst, in_=staged[:])
+                else:
+                    nc.scalar.activation(out=staged[:], in_=acc[:], func=ACT.Copy, scale=OUT_SCALE)
+                    (nc.scalar if last else nc.sync).dma_start(out=dst, in_=staged[:])
+
+        z_prev = weigh(0)
+        for c in range(1, n_chunks):
+            z_next = weigh(c)
+            score(c - 1, z_prev)
+            z_prev = z_next
+        score(n_chunks - 1, z_prev)

@@ -19,7 +19,7 @@ P = 128
 PACK = 4
 CHUNK = 128
 HALF = 256
-M_ON_SCALAR = 80
+M_HALF = HALF // PACK
 OUT_SCALE = 0.0625
 
 
@@ -33,17 +33,20 @@ def tile_picked_candhash_tanh_p_kernel(tc, x_words, x_scales, w1, gs, offs, cand
         cand_list = keep.tile([P, V // 16], U16, name="cand_list")
         table_words = keep.tile([P, T], U32, name="table_words")
         table_scales = keep.tile([P, T], U8, name="table_scales")
-        w_raw = keep.tile([P, PACK, H], F32, name="w_raw")
+        w_raw = [keep.tile([P, PACK, HALF], F32, name="w_raw%d" % u) for u in range(2)]
         gain = keep.tile([P, PACK], F32, name="gain")
 
+        words_hbm = x_words[0].rearrange("p n t -> p (n t)").bitcast(I32)
         nc.vector.memset(table_scales[:].bitcast(I32), 0)
-        nc.scalar.dma_start(out=w_raw[:], in_=w1.rearrange("(p j) c -> p j c", j=PACK))
-        nc.scalar.dma_start(out=table_words[:].bitcast(I32), in_=x_words[0].rearrange("p n t -> p (n t)").bitcast(I32))
+        w_hbm = w1.rearrange("(p j) c -> p j c", j=PACK)
+        nc.scalar.dma_start(out=w_raw[0][:], in_=w_hbm[:, :, :HALF])
         nc.sync.dma_start(offs_list[:], offs)
+        nc.sync.dma_start(cand_list[:], cand)
         scale_rows = x_scales[0].rearrange("(run r) n -> r run n", r=2)
         for r in range(2):
             nc.sync.dma_start(out=table_scales[r:P:16, :].bitcast(I32), in_=scale_rows[r].bitcast(I32))
-        nc.sync.dma_start(cand_list[:], cand)
+        nc.sync.dma_start(out=w_raw[1][:], in_=w_hbm[:, :, HALF:])
+        nc.sync.dma_start(out=table_words[:].bitcast(I32), in_=words_hbm)
         nc.sync.dma_start(out=gain[:], in_=gs.rearrange("(p t) o -> p (t o)", t=PACK))
 
         def picked_scales(index_list, label):
@@ -55,28 +58,28 @@ def tile_picked_candhash_tanh_p_kernel(tc, x_words, x_scales, w1, gs, offs, cand
                 nc.sync.dma_start(out=plane[2 + r : P : 32, :].bitcast(I32), in_=gathered[16 + r : P : 32, :].bitcast(I32))
             return plane
 
-        def picked_words(index_list, half, label):
-            words = keep.tile([P, HALF], U32, name="%s_words%d" % (label, half), align_bytes=64)
+        def picked_words(index_list, half, base):
+            words = picked[:, base + half * HALF : base + (half + 1) * HALF]
             cols = HALF // 16
-            nc.vector.tensor_copy(words[:], table_words[:].indirect(index_list[:, half * cols : (half + 1) * cols]))
+            nc.vector.tensor_copy(words, table_words[:].indirect(index_list[:, half * cols : (half + 1) * cols]))
             return words
 
         place_scales = picked_scales(offs_list, "place")
         cand_scales = picked_scales(cand_list, "cand")
 
-        w_grouped = keep.tile([P, PACK, P, PACK], BF16, name="w_grouped", align_bytes=64)
+        w_grouped = keep.tile([P, PACK, P, PACK], BF16, name="w_grouped", tag="grouped_then_picked", align_bytes=64)
         w_dst = w_grouped[:].rearrange("p t m j -> p m j t")
-        w_src = w_raw[:].rearrange("p j (m t) -> p m j t", t=PACK)
-        nc.scalar.copy(out=w_dst[:, :M_ON_SCALAR], in_=w_src[:, :M_ON_SCALAR])
-        nc.vector.tensor_copy(out=w_dst[:, M_ON_SCALAR:], in_=w_src[:, M_ON_SCALAR:])
+        for u in range(2):
+            nc.scalar.copy(out=w_dst[:, u * M_HALF : (u + 1) * M_HALF], in_=w_raw[u][:].rearrange("p j (m t) -> p m j t", t=PACK))
         w_codes = keep.tile([P, H], U32, name="w_codes", align_bytes=64)
         w_scales = keep.tile([P, H], U8, name="w_scales", align_bytes=64)
         nc.vector.quantize_mx(out=w_codes[:].bitcast(FP8X4), scales=w_scales[:], in_=w_grouped[:].rearrange("p t m j -> p (t m j)"))
 
+        picked = keep.tile([P, S + V], U32, name="picked", tag="grouped_then_picked", align_bytes=64)
         n_chunks = S // CHUNK
         hidden = []
         for half in range(2):
-            place_words = picked_words(offs_list, half, "place")
+            place_words = picked_words(offs_list, half, 0)
             for c in range(half * 2, half * 2 + 2):
                 acc = psum.tile([P, PACK, CHUNK], F32, name="h_acc%d" % c, tag="h_acc%d" % c)
                 local = (c % 2) * CHUNK
@@ -94,7 +97,7 @@ def tile_picked_candhash_tanh_p_kernel(tc, x_words, x_scales, w1, gs, offs, cand
                 nc.scalar.activation(out=h[:], in_=acc[:].rearrange("p t j -> p j t"), func=ACT.Tanh)
                 hidden.append(h)
 
-        cand_words = [picked_words(cand_list, half, "cand") for half in range(2)]
+        cand_words = [picked_words(cand_list, half, S) for half in range(2)]
         out_view = out.rearrange("(i p) j -> p i j", p=P)
 
         def weigh(c):

@@ -19,6 +19,7 @@ P = 128
 PACK = 4
 CHUNK = 128
 HALF = 256
+PIECE = 64
 M_HALF = HALF // PACK
 OUT_SCALE = 0.0625
 
@@ -42,9 +43,7 @@ def tile_picked_candhash_tanh_p_kernel(tc, x_words, x_scales, w1, gs, offs, cand
         nc.scalar.dma_start(out=w_raw[0][:], in_=w_hbm[:, :, :HALF])
         nc.sync.dma_start(offs_list[:], offs)
         nc.sync.dma_start(cand_list[:], cand)
-        scale_rows = x_scales[0].rearrange("(run r) n -> r run n", r=2)
-        for r in range(2):
-            nc.sync.dma_start(out=table_scales[r:P:16, :].bitcast(I32), in_=scale_rows[r].bitcast(I32))
+        nc.sync.dma_start(out=table_scales[0:P:8, :].bitcast(I32), in_=x_scales[0].bitcast(I32))
         nc.sync.dma_start(out=w_raw[1][:], in_=w_hbm[:, :, HALF:])
         nc.sync.dma_start(out=table_words[:].bitcast(I32), in_=words_hbm)
         nc.sync.dma_start(out=gain[:], in_=gs.rearrange("(p t) o -> p (t o)", t=PACK))
@@ -52,10 +51,10 @@ def tile_picked_candhash_tanh_p_kernel(tc, x_words, x_scales, w1, gs, offs, cand
         def picked_scales(index_list, label):
             gathered = keep.tile([P, S], U8, name=label + "_gathered")
             plane = keep.tile([P, S], U8, name=label + "_plane", align_bytes=64)
+            nc.vector.memset(plane[:].bitcast(I32), 0)
             nc.vector.tensor_copy(gathered[:], table_scales[:].indirect(index_list[:]))
-            nc.vector.tensor_copy(plane[:].bitcast(I32), gathered[:].bitcast(I32))
-            for r in range(2):
-                nc.sync.dma_start(out=plane[2 + r : P : 32, :].bitcast(I32), in_=gathered[16 + r : P : 32, :].bitcast(I32))
+            for b in range(4):
+                nc.sync.dma_start(out=plane[b:P:32, :].bitcast(I32), in_=gathered[8 * b : P : 32, :].bitcast(I32))
             return plane
 
         def picked_words(index_list, half, base):
@@ -100,43 +99,50 @@ def tile_picked_candhash_tanh_p_kernel(tc, x_words, x_scales, w1, gs, offs, cand
         cand_words = [picked_words(cand_list, half, S) for half in range(2)]
         out_view = out.rearrange("(i p) j -> p i j", p=P)
 
-        def weigh(c):
-            z = keep.tile([P, CHUNK, PACK], BF16, name="z%d" % c, align_bytes=64)
-            nc.vector.tensor_tensor(out=z[:], in0=hidden[c][:], in1=gain[:].unsqueeze(1).to_broadcast([P, CHUNK, PACK]), op=MULT)
-            return z
+        z = [keep.tile([P, CHUNK, PACK], BF16, name="z%d" % c, align_bytes=64) for c in range(n_chunks)]
+        z_codes = [keep.tile([P, CHUNK], U32, name="z_codes%d" % c, align_bytes=64) for c in range(n_chunks)]
+        z_scales = [keep.tile([P, CHUNK], U8, name="z_scales%d" % c, align_bytes=64) for c in range(n_chunks)]
 
-        def score(c, z):
-            z_codes = keep.tile([P, CHUNK], U32, name="z_codes%d" % c, align_bytes=64)
-            z_scales = keep.tile([P, CHUNK], U8, name="z_scales%d" % c, align_bytes=64)
-            nc.vector.quantize_mx(out=z_codes[:].bitcast(FP8X4), scales=z_scales[:], in_=z[:].rearrange("p j t -> p (j t)"))
-            last = c == n_chunks - 1
-            groups = [(0, 2), (2, 4)] if last else [(0, 4)]
-            for g, (i0, i1) in enumerate(groups):
-                tag = "h_acc0" if g == 1 else "o_acc%d" % c
-                acc = psum.tile([P, i1 - i0, CHUNK], F32, name="o_acc%d_%d" % (c, g), tag=tag)
-                for i in range(i0, i1):
-                    local = (i % 2) * P
+        def piece_cols(piece):
+            c, u = divmod(piece, CHUNK // PIECE)
+            return c, slice(u * PIECE, (u + 1) * PIECE)
+
+        def weigh(piece):
+            c, cols = piece_cols(piece)
+            nc.vector.tensor_tensor(out=z[c][:, cols, :], in0=hidden[c][:, cols, :], in1=gain[:].unsqueeze(1).to_broadcast([P, PIECE, PACK]), op=MULT)
+
+        def quantise(piece):
+            c, cols = piece_cols(piece)
+            nc.vector.quantize_mx(out=z_codes[c][:, cols].bitcast(FP8X4), scales=z_scales[c][:, cols], in_=z[c][:, cols, :].rearrange("p j t -> p (j t)"))
+
+        def score(c):
+            for g in range(2):
+                bank = 2 * c + g
+                tag = "o_acc%d" % bank if bank < n_chunks else "h_acc%d" % (bank - n_chunks)
+                acc = psum.tile([P, 2, CHUNK], F32, name="o_acc%d" % bank, tag=tag)
+                for i in range(2):
                     nc.tensor.matmul_mx(
-                        out=acc[:, i - i0, :],
-                        lhsT=cand_words[i // 2][:, local : local + P].bitcast(FP8X4),
-                        lhsT_scale=cand_scales[:, i * P : (i + 1) * P],
-                        rhs=z_codes[:].bitcast(FP8X4),
-                        rhs_scale=z_scales[:],
+                        out=acc[:, i, :],
+                        lhsT=cand_words[g][:, i * P : (i + 1) * P].bitcast(FP8X4),
+                        lhsT_scale=cand_scales[:, (2 * g + i) * P : (2 * g + i + 1) * P],
+                        rhs=z_codes[c][:].bitcast(FP8X4),
+                        rhs_scale=z_scales[c][:],
                         start=True,
                         stop=True,
                     )
-                staged = keep.tile([P, i1 - i0, CHUNK], F32, name="staged%d_%d" % (c, g))
-                dst = out_view[:, i0:i1, c * CHUNK : (c + 1) * CHUNK]
-                if g == 1:
+                staged = keep.tile([P, 2, CHUNK], F32, name="staged%d" % bank)
+                dst = out_view[:, 2 * g : 2 * g + 2, c * CHUNK : (c + 1) * CHUNK]
+                if bank == 2 * n_chunks - 1:
                     nc.vector.tensor_scalar_mul(out=staged[:], in0=acc[:], scalar1=OUT_SCALE)
-                    nc.sync.dma_start(out=dst, in_=staged[:])
                 else:
                     nc.scalar.activation(out=staged[:], in_=acc[:], func=ACT.Copy, scale=OUT_SCALE)
-                    (nc.scalar if last else nc.sync).dma_start(out=dst, in_=staged[:])
+                nc.sync.dma_start(out=dst, in_=staged[:])
 
-        z_prev = weigh(0)
-        for c in range(1, n_chunks):
-            z_next = weigh(c)
-            score(c - 1, z_prev)
-            z_prev = z_next
-        score(n_chunks - 1, z_prev)
+        n_pieces = S // PIECE
+        weigh(0)
+        for piece in range(n_pieces):
+            if piece + 1 < n_pieces:
+                weigh(piece + 1)
+            quantise(piece)
+            if piece % 2 == 1:
+                score(piece // 2)

@@ -41,12 +41,12 @@ def tile_picked_candhash_tanh_p_kernel(tc, x_words, x_scales, w1, gs, offs, cand
         nc.vector.memset(table_scales[:].bitcast(I32), 0)
         w_hbm = w1.rearrange("(p j) c -> p j c", j=PACK)
         nc.scalar.dma_start(out=w_raw[0][:], in_=w_hbm[:, :, :HALF])
+        nc.scalar.dma_start(out=gain[:], in_=gs.rearrange("(p t) o -> p (t o)", t=PACK))
         nc.sync.dma_start(offs_list[:], offs)
         nc.sync.dma_start(cand_list[:], cand)
         nc.sync.dma_start(out=table_scales[0:P:8, :].bitcast(I32), in_=x_scales[0].bitcast(I32))
         nc.sync.dma_start(out=w_raw[1][:], in_=w_hbm[:, :, HALF:])
         nc.sync.dma_start(out=table_words[:].bitcast(I32), in_=words_hbm)
-        nc.sync.dma_start(out=gain[:], in_=gs.rearrange("(p t) o -> p (t o)", t=PACK))
 
         def picked_scales(index_list, label):
             gathered = keep.tile([P, S], U8, name=label + "_gathered")
@@ -93,56 +93,61 @@ def tile_picked_candhash_tanh_p_kernel(tc, x_words, x_scales, w1, gs, offs, cand
                         stop=True,
                     )
                 h = keep.tile([P, CHUNK, PACK], F32, name="h%d" % c)
-                nc.scalar.activation(out=h[:], in_=acc[:].rearrange("p t j -> p j t"), func=ACT.Tanh)
+                step = PIECE if c == 0 else CHUNK
+                for lo in range(0, CHUNK, step):
+                    nc.scalar.activation(out=h[:, lo : lo + step], in_=acc[:, :, lo : lo + step].rearrange("p t j -> p j t"), func=ACT.Tanh)
                 hidden.append(h)
 
-        cand_words = [picked_words(cand_list, half, S) for half in range(2)]
+        cand_words = picked[:, S:]
+        nc.vector.tensor_copy(cand_words, table_words[:].indirect(cand_list[:]))
         out_view = out.rearrange("(i p) j -> p i j", p=P)
 
-        z = [keep.tile([P, CHUNK, PACK], BF16, name="z%d" % c, align_bytes=64) for c in range(n_chunks)]
-        z_codes = [keep.tile([P, CHUNK], U32, name="z_codes%d" % c, align_bytes=64) for c in range(n_chunks)]
-        z_scales = [keep.tile([P, CHUNK], U8, name="z_scales%d" % c, align_bytes=64) for c in range(n_chunks)]
-
-        def piece_cols(piece):
-            c, u = divmod(piece, CHUNK // PIECE)
-            return c, slice(u * PIECE, (u + 1) * PIECE)
+        z = keep.tile([P, S, PACK], BF16, name="z", align_bytes=64)
+        z_codes = keep.tile([P, S], U32, name="z_codes", align_bytes=64)
+        z_scales = keep.tile([P, S], U8, name="z_scales", align_bytes=64)
+        n_pieces = S // PIECE
+        free_banks = ["o_acc%d" % b for b in range(n_chunks)] + ["h_acc%d" % b for b in range(n_chunks)]
 
         def weigh(piece):
-            c, cols = piece_cols(piece)
-            nc.vector.tensor_tensor(out=z[c][:, cols, :], in0=hidden[c][:, cols, :], in1=gain[:].unsqueeze(1).to_broadcast([P, PIECE, PACK]), op=MULT)
+            c, u = divmod(piece, CHUNK // PIECE)
+            nc.vector.tensor_tensor(
+                out=z[:, piece * PIECE : (piece + 1) * PIECE, :],
+                in0=hidden[c][:, u * PIECE : (u + 1) * PIECE, :],
+                in1=gain[:].unsqueeze(1).to_broadcast([P, PIECE, PACK]),
+                op=MULT,
+            )
 
         def quantise(piece):
-            c, cols = piece_cols(piece)
-            nc.vector.quantize_mx(out=z_codes[c][:, cols].bitcast(FP8X4), scales=z_scales[c][:, cols], in_=z[c][:, cols, :].rearrange("p j t -> p (j t)"))
+            cols = slice(piece * PIECE, (piece + 1) * PIECE)
+            nc.vector.quantize_mx(out=z_codes[:, cols].bitcast(FP8X4), scales=z_scales[:, cols], in_=z[:, cols, :].rearrange("p j t -> p (j t)"))
 
-        def score(c):
-            for g in range(2):
-                bank = 2 * c + g
-                tag = "o_acc%d" % bank if bank < n_chunks else "h_acc%d" % (bank - n_chunks)
-                acc = psum.tile([P, 2, CHUNK], F32, name="o_acc%d" % bank, tag=tag)
-                for i in range(2):
-                    nc.tensor.matmul_mx(
-                        out=acc[:, i, :],
-                        lhsT=cand_words[g][:, i * P : (i + 1) * P].bitcast(FP8X4),
-                        lhsT_scale=cand_scales[:, (2 * g + i) * P : (2 * g + i + 1) * P],
-                        rhs=z_codes[c][:].bitcast(FP8X4),
-                        rhs_scale=z_scales[c][:],
-                        start=True,
-                        stop=True,
-                    )
-                staged = keep.tile([P, 2, CHUNK], F32, name="staged%d" % bank)
-                dst = out_view[:, 2 * g : 2 * g + 2, c * CHUNK : (c + 1) * CHUNK]
-                if bank == 2 * n_chunks - 1:
-                    nc.vector.tensor_scalar_mul(out=staged[:], in0=acc[:], scalar1=OUT_SCALE)
-                else:
-                    nc.scalar.activation(out=staged[:], in_=acc[:], func=ACT.Copy, scale=OUT_SCALE)
-                nc.sync.dma_start(out=dst, in_=staged[:])
+        def score(cols, row_tiles, on_vector):
+            width = cols.stop - cols.start
+            label = "%d_%d" % (cols.start, row_tiles[0])
+            acc = psum.tile([P, len(row_tiles), width], F32, name="o_acc" + label, tag=free_banks.pop(0))
+            for slot, i in enumerate(row_tiles):
+                nc.tensor.matmul_mx(
+                    out=acc[:, slot, :],
+                    lhsT=cand_words[:, i * P : (i + 1) * P].bitcast(FP8X4),
+                    lhsT_scale=cand_scales[:, i * P : (i + 1) * P],
+                    rhs=z_codes[:, cols].bitcast(FP8X4),
+                    rhs_scale=z_scales[:, cols],
+                    start=True,
+                    stop=True,
+                )
+            staged = keep.tile([P, len(row_tiles), width], F32, name="staged" + label)
+            if on_vector:
+                nc.vector.tensor_scalar_mul(out=staged[:], in0=acc[:], scalar1=OUT_SCALE)
+            else:
+                nc.scalar.activation(out=staged[:], in_=acc[:], func=ACT.Copy, scale=OUT_SCALE)
+            nc.sync.dma_start(out=out_view[:, row_tiles[0] : row_tiles[-1] + 1, cols], in_=staged[:])
 
-        n_pieces = S // PIECE
         weigh(0)
         for piece in range(n_pieces):
             if piece + 1 < n_pieces:
                 weigh(piece + 1)
             quantise(piece)
             if piece % 2 == 1:
-                score(piece // 2)
+                cols = slice((piece - 1) * PIECE, (piece + 1) * PIECE)
+                score(cols, (0, 1), False)
+                score(cols, (2, 3), piece >= n_pieces - 3)

from contextlib import ExitStack

import concourse.mybir as mybir

K, T, S, V, H = 512, 2048, 512, 512, 512
FLOPS = 2 * K * H * S + 2 * K * V * S

F32 = mybir.dt.float32
BF16 = mybir.dt.bfloat16
I32 = mybir.dt.int32
U32 = mybir.dt.uint32
U16 = mybir.dt.uint16
U8 = mybir.dt.uint8
FP8X4 = mybir.dt.float8_e4m3fn_x4
ACT = mybir.ActivationFunctionType
MULT = mybir.AluOpType.mult

P = 128
PACK = 4
CHUNK = 128
HALF = 256
PIECE = 64
M_HALF = HALF // PACK
OUT_SCALE = 0.0625


def tile_picked_candhash_tanh_p_kernel(tc, x_words, x_scales, w1, gs, offs, cand, out):
    nc = tc.nc
    with ExitStack() as ctx:
        keep = ctx.enter_context(tc.tile_pool(name="keep", bufs=1))
        psum = ctx.enter_context(tc.psum_pool(name="psum", bufs=1))

        offs_list = keep.tile([P, S // 16], U16, name="offs_list")
        cand_list = keep.tile([P, V // 16], U16, name="cand_list")
        table_words = keep.tile([P, T], U32, name="table_words")
        table_scales = keep.tile([P, T], U8, name="table_scales")
        w_raw = [keep.tile([P, PACK, HALF], F32, name="w_raw%d" % u) for u in range(2)]
        gain = keep.tile([P, PACK], F32, name="gain")

        words_hbm = x_words[0].rearrange("p n t -> p (n t)").bitcast(I32)
        nc.vector.memset(table_scales[:].bitcast(I32), 0)
        w_hbm = w1.rearrange("(p j) c -> p j c", j=PACK)
        nc.scalar.dma_start(out=w_raw[0][:], in_=w_hbm[:, :, :HALF])
        nc.scalar.dma_start(out=gain[:], in_=gs.rearrange("(p t) o -> p (t o)", t=PACK))
        nc.sync.dma_start(offs_list[:], offs)
        nc.sync.dma_start(cand_list[:], cand)
        nc.sync.dma_start(out=table_scales[0:P:8, :].bitcast(I32), in_=x_scales[0].bitcast(I32))
        nc.sync.dma_start(out=w_raw[1][:], in_=w_hbm[:, :, HALF:])
        nc.sync.dma_start(out=table_words[:].bitcast(I32), in_=words_hbm)

        def picked_scales(index_list, label):
            gathered = keep.tile([P, S], U8, name=label + "_gathered")
            plane = keep.tile([P, S], U8, name=label + "_plane", align_bytes=64)
            nc.vector.memset(plane[:].bitcast(I32), 0)
            nc.vector.tensor_copy(gathered[:], table_scales[:].indirect(index_list[:]))
            for b in range(4):
                nc.sync.dma_start(out=plane[b:P:32, :].bitcast(I32), in_=gathered[8 * b : P : 32, :].bitcast(I32))
            return plane

        def picked_words(index_list, half, base):
            words = picked[:, base + half * HALF : base + (half + 1) * HALF]
            cols = HALF // 16
            nc.vector.tensor_copy(words, table_words[:].indirect(index_list[:, half * cols : (half + 1) * cols]))
            return words

        place_scales = picked_scales(offs_list, "place")
        cand_scales = picked_scales(cand_list, "cand")

        w_grouped = keep.tile([P, PACK, P, PACK], BF16, name="w_grouped", tag="grouped_then_picked", align_bytes=64)
        w_dst = w_grouped[:].rearrange("p t m j -> p m j t")
        for u in range(2):
            nc.scalar.copy(out=w_dst[:, u * M_HALF : (u + 1) * M_HALF], in_=w_raw[u][:].rearrange("p j (m t) -> p m j t", t=PACK))
        w_codes = keep.tile([P, H], U32, name="w_codes", align_bytes=64)
        w_scales = keep.tile([P, H], U8, name="w_scales", align_bytes=64)
        nc.vector.quantize_mx(out=w_codes[:].bitcast(FP8X4), scales=w_scales[:], in_=w_grouped[:].rearrange("p t m j -> p (t m j)"))

        picked = keep.tile([P, S + V], U32, name="picked", tag="grouped_then_picked", align_bytes=64)
        n_chunks = S // CHUNK
        hidden = []
        for half in range(2):
            place_words = picked_words(offs_list, half, 0)
            for c in range(half * 2, half * 2 + 2):
                acc = psum.tile([P, PACK, CHUNK], F32, name="h_acc%d" % c, tag="h_acc%d" % c)
                local = (c % 2) * CHUNK
                for t in range(PACK):
                    nc.tensor.matmul_mx(
                        out=acc[:, t, :],
                        lhsT=w_codes[:, t * P : (t + 1) * P].bitcast(FP8X4),
                        lhsT_scale=w_scales[:, t * P : (t + 1) * P],
                        rhs=place_words[:, local : local + CHUNK].bitcast(FP8X4),
                        rhs_scale=place_scales[:, c * CHUNK : (c + 1) * CHUNK],
                        start=True,
                        stop=True,
                    )
                h = keep.tile([P, CHUNK, PACK], F32, name="h%d" % c)
                step = PIECE if c == 0 else CHUNK
                for lo in range(0, CHUNK, step):
                    nc.scalar.activation(out=h[:, lo : lo + step], in_=acc[:, :, lo : lo + step].rearrange("p t j -> p j t"), func=ACT.Tanh)
                hidden.append(h)

        cand_words = picked[:, S:]
        nc.vector.tensor_copy(cand_words, table_words[:].indirect(cand_list[:]))
        out_view = out.rearrange("(i p) j -> p i j", p=P)

        z = keep.tile([P, S, PACK], BF16, name="z", align_bytes=64)
        z_codes = keep.tile([P, S], U32, name="z_codes", align_bytes=64)
        z_scales = keep.tile([P, S], U8, name="z_scales", align_bytes=64)
        n_pieces = S // PIECE
        free_banks = ["o_acc%d" % b for b in range(n_chunks)] + ["h_acc%d" % b for b in range(n_chunks)]

        def weigh(piece):
            c, u = divmod(piece, CHUNK // PIECE)
            nc.vector.tensor_tensor(
                out=z[:, piece * PIECE : (piece + 1) * PIECE, :],
                in0=hidden[c][:, u * PIECE : (u + 1) * PIECE, :],
                in1=gain[:].unsqueeze(1).to_broadcast([P, PIECE, PACK]),
                op=MULT,
            )

        def quantise(piece):
            cols = slice(piece * PIECE, (piece + 1) * PIECE)
            nc.vector.quantize_mx(out=z_codes[:, cols].bitcast(FP8X4), scales=z_scales[:, cols], in_=z[:, cols, :].rearrange("p j t -> p (j t)"))

        def score(cols, row_tiles, on_vector):
            width = cols.stop - cols.start
            label = "%d_%d" % (cols.start, row_tiles[0])
            acc = psum.tile([P, len(row_tiles), width], F32, name="o_acc" + label, tag=free_banks.pop(0))
            for slot, i in enumerate(row_tiles):
                nc.tensor.matmul_mx(
                    out=acc[:, slot, :],
                    lhsT=cand_words[:, i * P : (i + 1) * P].bitcast(FP8X4),
                    lhsT_scale=cand_scales[:, i * P : (i + 1) * P],
                    rhs=z_codes[:, cols].bitcast(FP8X4),
                    rhs_scale=z_scales[:, cols],
                    start=True,
                    stop=True,
                )
            staged = keep.tile([P, len(row_tiles), width], F32, name="staged" + label)
            if on_vector:
                nc.vector.tensor_scalar_mul(out=staged[:], in0=acc[:], scalar1=OUT_SCALE)
            else:
                nc.scalar.activation(out=staged[:], in_=acc[:], func=ACT.Copy, scale=OUT_SCALE)
            nc.sync.dma_start(out=out_view[:, row_tiles[0] : row_tiles[-1] + 1, cols], in_=staged[:])

        weigh(0)
        for piece in range(n_pieces):
            if piece + 1 < n_pieces:
                weigh(piece + 1)
            quantise(piece)
            if piece % 2 == 1:
                cols = slice((piece - 1) * PIECE, (piece + 1) * PIECE)
                score(cols, (0, 1), False)
                score(cols, (2, 3), piece >= n_pieces - 3)
